import numpy as np
import ml_dtypes


def mxq(x, axis, fmt="e4m3"):
    dtype, down = {"e4m3": (ml_dtypes.float8_e4m3fn, 7), "e5m2": (ml_dtypes.float8_e5m2, 14)}[fmt]
    v = np.moveaxis(np.asarray(x, np.float32).astype(ml_dtypes.bfloat16).astype(np.float64), axis, -1)
    blocks = v.reshape(v.shape[:-1] + (-1, 32))
    amax = np.abs(blocks).max(-1, keepdims=True)
    byte = np.maximum(np.where(amax > 0, np.frexp(amax)[1] - 1 + 127, 0) - down, 1)
    scale = np.exp2(byte - 127.0)
    codes = (blocks / scale).astype(np.float32).astype(dtype).astype(np.float64)
    return np.moveaxis((codes * scale).reshape(v.shape), -1, axis)


WIDE = False


def mx_kscale(k):
    if not WIDE:
        return np.ones(k)
    levels = np.array([10, -10, 5, -5, 0])
    if k % 512:
        return np.exp2(np.random.permutation(np.resize(levels, k // 32))).repeat(32)
    a = np.empty((k // 512, 16))
    for p in range(k // 512):
        a[p, :8] = np.random.permutation(np.resize(levels, 8))
        for g in range(8):
            far = levels[np.abs(levels - a[p, g]) >= 10]
            a[p, g + 8] = far[np.random.randint(len(far))]
    return np.exp2(a.ravel()).repeat(32)


def f64(x):
    return np.asarray(x).astype(np.float64)


def striped(idx):
    return np.tile(idx.reshape(-1, 16).T, (8, 1)).astype(np.uint16)


def unstriped(offs):
    return offs[:16].T.reshape(-1).astype(np.int64)


E2M1 = np.array([0.0, 0.5, 1.0, 1.5, 2.0, 3.0, 4.0, 6.0, -0.0, -0.5, -1.0, -1.5, -2.0, -3.0, -4.0, -6.0])


def pack_weight(w, fmt):
    k, n = w.shape
    w = f64(np.asarray(w, np.float32).astype(ml_dtypes.bfloat16)).reshape(k // 32, 32, n)
    amax = np.abs(w).max(1)
    if fmt == "e4m3":
        byte = np.frexp(amax)[1] - 1 + 127 - 7
    else:
        mant, ex = np.frexp(amax / 6.0)
        byte = np.where(mant > 0.5, ex, ex - 1) + 127
    byte = np.clip(np.where(amax > 0, byte, 1), 1, 254)
    scaled = (w * np.exp2(127.0 - byte)[:, None, :]).reshape(k, n).astype(np.float32)
    by_word = np.ascontiguousarray(scaled.reshape(k // 512, 128, 4, n).transpose(0, 1, 3, 2))
    if fmt == "e4m3":
        words = by_word.astype(ml_dtypes.float8_e4m3fn).view(np.uint8)
    else:
        c = by_word.astype(ml_dtypes.float4_e2m1fn).view(np.uint8) & 0xF
        words = (c[..., 0::2] | (c[..., 1::2] << 4)).reshape(k // 512, 128, 2 * n)
    return np.ascontiguousarray(words), np.ascontiguousarray(byte.astype(np.uint8).reshape(k // 512, 16, n))


def unpack_weight(words, scales, fmt):
    g, _, n = scales.shape
    words = np.ascontiguousarray(words).reshape(g, 128, n, -1)
    if fmt == "e4m3":
        vals = words.view(ml_dtypes.float8_e4m3fn).astype(np.float64)
    else:
        nib = np.empty((g, 128, n, 4), np.uint8)
        nib[..., 0::2] = words & 0xF
        nib[..., 1::2] = words >> 4
        vals = E2M1[nib]
    vals = vals * np.repeat(np.exp2(scales.astype(np.float64) - 127.0), 8, axis=1)[..., None]
    return vals.transpose(0, 1, 3, 2).reshape(g * 512, n)


def gelu(v):
    return 0.5 * v * (1.0 + np.tanh(np.sqrt(2.0 / np.pi) * (v + 0.044715 * v**3)))


K, KB, T, S, H, T3, S2, T2 = 1024, 512, 4096, 1024, 1024, 2048, 512, 2048

def setup_inputs():
    n = np.random.standard_normal
    s = u = mx_kscale(K)[:, None]
    tab_words, tab_scales = pack_weight(2.0 * n((K, T)) * s, "e4m3")
    tab2_words, tab2_scales = pack_weight(n((H, T3)) / np.sqrt(H) / u, "e4m3")
    w4_words, w4_scales = pack_weight(0.75 * n((KB, H)) / np.sqrt(K) / s[:KB], "e2m1")
    return {
        "tab_words": tab_words, "tab_scales": tab_scales,
        "offs": striped(np.random.permutation(T)[:S]),
        "tab2_words": tab2_words, "tab2_scales": tab2_scales,
        "offs2": striped(np.random.permutation(T3)[:S2]),
        "offs3": striped(np.random.permutation(T2)[:S]),
        "w4_words": w4_words, "w4_scales": w4_scales,
        "w1": (0.75 * n((K - KB, H)) / np.sqrt(K) / s[KB:]).astype(np.float32),
        "gain": (1.5 * np.exp(0.3 * n(H)) * u[:, 0]).astype(np.float32),
        "hand": (0.8 * n((H, S)) * u).astype(np.float32),
        "breed": (0.5 * n(S2)).astype(np.float32),
        "wgo": np.exp(0.3 * n((128, S))).astype(np.float32),
        "page1": (0.6 * n((S2, T2))).astype(np.float32),
    }

def reference(tab_words, tab_scales, offs, tab2_words, tab2_scales, offs2, offs3,
              w4_words, w4_scales, w1, gain, hand, breed, wgo, page1):
    v = unpack_weight(tab_words, tab_scales, "e4m3")[:, unstriped(offs)]
    v2 = unpack_weight(tab2_words, tab2_scales, "e4m3")[:, unstriped(offs2)]
    w4 = unpack_weight(w4_words, w4_scales, "e2m1")
    wc = mxq(f64(w1), 0, "e4m3")
    x = w4.T @ v[:KB] + wc.T @ v[KB:]
    h = f64(gain)[:, None] * np.tanh(x) + f64(hand)
    hq = mxq(h, 0, "e4m3")
    e = v2.T @ hq
    d = v2.T @ v
    y = e * (1.0 / (1.0 + np.exp(-d))) + f64(breed)[:, None]
    out = f64(page1).copy()
    out[:, unstriped(offs3)] = np.tile(f64(wgo), (S2 // 128, 1)) * y
    return out

@@ -1,0 +1,259 @@
+from contextlib import ExitStack
+
+import concourse.mybir as mybir
+
+K, KB, T, S, H, T3, S2, T2 = 1024, 512, 4096, 1024, 1024, 2048, 512, 2048
+FLOPS = 2 * K * H * S + 2 * 2 * H * S2 * S
+
+F32 = mybir.dt.float32
+BF16 = mybir.dt.bfloat16
+I32 = mybir.dt.int32
+U32 = mybir.dt.uint32
+U16 = mybir.dt.uint16
+U8 = mybir.dt.uint8
+FP8X4 = mybir.dt.float8_e4m3fn_x4
+FP4X4 = mybir.dt.float4_e2m1fn_x4
+ACT = mybir.ActivationFunctionType
+ALU = mybir.AluOpType
+
+P = 128
+PACK = 4
+PASS = P * PACK
+PASSES = 2
+N = 512
+HALVES = S // N
+M_TILES = S2 // P
+LIST_COLS = N // 16
+STD_RUN = 256
+
+
+def tile_list_steward_ring_scores_kernel(
+    tc, tab_words, tab_scales, offs, tab2_words, tab2_scales, offs2, offs3,
+    w4_words, w4_scales, w1, gain, hand, breed, wgo, page1, out,
+):
+    nc = tc.nc
+    with ExitStack() as ctx:
+        keep = ctx.enter_context(tc.tile_pool(name="keep", bufs=1))
+        work = ctx.enter_context(tc.tile_pool(name="work", bufs=2))
+        psum = ctx.enter_context(tc.psum_pool(name="psum", bufs=1))
+
+        def held(name, shape, dtype):
+            return keep.tile(shape, dtype, name=name, align_bytes=64)
+
+        cat_list = held("cat_list", [P, S // 16], U16)
+        std_list = held("std_list", [P, S2 // 16], U16)
+        col_list = held("col_list", [P, S // 16], U16)
+        cat_tab = [held("cat_tab%d" % a, [P, T], U32) for a in range(PASSES)]
+        cat_tab_sc = held("cat_tab_sc", [P, T], U8)
+        std_tab = [held("std_tab%d" % a, [P, T3], U32) for a in range(PASSES)]
+        std_tab_sc = held("std_tab_sc", [P, T3], U8)
+        w4_raw = held("w4_raw", [P, 2 * H], U8)
+        w4_raw_sc = held("w4_raw_sc", [P, H], U8)
+        w4 = held("w4", [P, 2 * H], U8)
+        w4_sc = held("w4_sc", [P, H], U8)
+        w1_raw = [held("w1_raw%d" % b, [P, PACK, PASS], F32) for b in range(PASSES)]
+        w1_bf = [held("w1_bf%d" % b, [P, PASS * PACK], BF16) for b in range(PASSES)]
+        w1_q = [held("w1_q%d" % b, [P, PASS], U32) for b in range(PASSES)]
+        w1_sc = [held("w1_sc%d" % b, [P, PASS], U8) for b in range(PASSES)]
+        gain_sb = held("gain_sb", [P, PASSES, PACK], F32)
+        breed_sb = held("breed_sb", [P, M_TILES], F32)
+        hand_sb = {(j, b): held("hand%d_%d" % (j, b), [P, PACK, N], F32) for j in range(HALVES) for b in range(PASSES)}
+        wgo_sb = [held("wgo%d" % j, [P, N], F32) for j in range(HALVES)]
+        page = [held("page%d" % m, [P, T2], F32) for m in range(M_TILES)]
+        cat = {(a, j): held("cat%d_%d" % (a, j), [P, N], U32) for a in range(PASSES) for j in range(HALVES)}
+        cat_sc = [held("cat_sc%d" % j, [P, N], U8) for j in range(HALVES)]
+        std = [held("std%d" % a, [P, S2], U32) for a in range(PASSES)]
+        std_sc = held("std_sc", [P, S2], U8)
+        h_q = {(j, b): held("h_q%d_%d" % (j, b), [P, N], U32) for j in range(HALVES) for b in range(PASSES)}
+        h_sc = {(j, b): held("h_sc%d_%d" % (j, b), [P, N], U8) for j in range(HALVES) for b in range(PASSES)}
+
+        def load_words(tile, words):
+            nc.sync.dma_start(out=tile[:].bitcast(I32), in_=words.rearrange("p t i -> p (t i)").bitcast(I32))
+
+        def load_scales(queue, tile, scales):
+            passes = scales.shape[0]
+            for q in range(4):
+                queue.dma_start(
+                    out=tile[32 * q : 32 * q + 4 * passes, :].bitcast(I32),
+                    in_=scales[:, 4 * q : 4 * q + 4, :].bitcast(I32),
+                )
+
+        def load_pass_scales(tile, scales, a):
+            for q in range(4):
+                row = 32 * q + 4 * a
+                nc.sync.dma_start(out=tile[row : row + 4, :].bitcast(I32), in_=scales[a, 4 * q : 4 * q + 4, :].bitcast(I32))
+
+        def load_w1(b):
+            nc.sync.dma_start(out=w1_raw[b][:], in_=w1[:, b * PASS : (b + 1) * PASS].rearrange("(p i) c -> p i c", i=PACK))
+
+        def load_hand(j, b):
+            rows = hand[b * PASS : (b + 1) * PASS, j * N : (j + 1) * N]
+            nc.sync.dma_start(out=hand_sb[j, b][:], in_=rows.rearrange("(p t) n -> p t n", t=PACK))
+
+        def load_wgo(j):
+            nc.sync.dma_start(out=wgo_sb[j][:], in_=wgo[:, j * N : (j + 1) * N])
+
+        def load_page(m):
+            nc.sync.dma_start(out=page[m][:], in_=page1[m * P : (m + 1) * P, :])
+
+        nc.gpsimd.memset(cat_tab_sc[:, 0 : T // 2].bitcast(I32), 0)
+        nc.vector.memset(cat_tab_sc[:, T // 2 : T].bitcast(I32), 0)
+        for tile in (std_tab_sc, w4_raw_sc):
+            nc.vector.memset(tile[:].bitcast(I32), 0)
+        nc.sync.dma_start(cat_list[:], offs)
+        nc.sync.dma_start(out=w4_raw[:].bitcast(I32), in_=w4_words[0].bitcast(I32))
+        load_words(cat_tab[0], tab_words[0])
+        load_pass_scales(cat_tab_sc, tab_scales, 0)
+        nc.sync.dma_start(out=gain_sb[:], in_=gain.rearrange("(b p t) -> p b t", b=PASSES, t=PACK))
+        load_scales(nc.gpsimd, std_tab_sc, tab2_scales)
+        load_w1(0)
+        load_pass_scales(cat_tab_sc, tab_scales, 1)
+        load_w1(1)
+        load_scales(nc.sync, w4_raw_sc, w4_scales)
+        load_words(cat_tab[1], tab_words[1])
+        nc.sync.dma_start(std_list[:], offs2)
+        load_words(std_tab[0], tab2_words[0])
+        load_hand(0, 0)
+        load_words(std_tab[1], tab2_words[1])
+        load_hand(0, 1)
+        load_hand(1, 0)
+        nc.sync.dma_start(col_list[:], offs3)
+        load_wgo(0)
+        with nc.allow_non_contiguous_dma(reason="one bias value a partition"):
+            nc.sync.dma_start(out=breed_sb[:], in_=breed.rearrange("(m p) -> p m", p=P))
+        load_page(0)
+        load_page(1)
+        load_hand(1, 1)
+        load_page(2)
+        load_page(3)
+        load_wgo(1)
+
+        def deal_w4_words():
+            nc.vector.tensor_copy(
+                out=w4[:].rearrange("p (b t q y) -> p b t q y", b=PASSES, t=PACK, y=2),
+                in_=w4_raw[:].rearrange("p (b q t y) -> p b t q y", b=PASSES, t=PACK, y=2),
+            )
+
+        def deal_w4_scales():
+            nc.vector.tensor_copy(
+                out=w4_sc[:].rearrange("p (b t q) -> p b t q", b=PASSES, t=PACK),
+                in_=w4_raw_sc[:].rearrange("p (b q t) -> p b t q", b=PASSES, t=PACK),
+            )
+
+        def round_w1(b):
+            nc.scalar.copy(
+                out=w1_bf[b][:].rearrange("p (t q i) -> p q t i", t=PACK, i=PACK),
+                in_=w1_raw[b][:].rearrange("p i (q t) -> p q t i", t=PACK),
+            )
+
+        def quantize_w1(b):
+            nc.vector.quantize_mx(out=w1_q[b][:].bitcast(FP8X4), scales=w1_sc[b][:], in_=w1_bf[b][:])
+
+        def gather_cats(dst, table, j):
+            nc.vector.tensor_copy(dst[:], table[:].indirect(cat_list[:, j * LIST_COLS : (j + 1) * LIST_COLS]))
+
+        def gather_standards(dst, table):
+            cols = STD_RUN // 16
+            for u in range(S2 // STD_RUN):
+                nc.vector.tensor_copy(
+                    dst[:, u * STD_RUN : (u + 1) * STD_RUN], table[:].indirect(std_list[:, u * cols : (u + 1) * cols])
+                )
+
+        def features(j, b):
+            planes = work.tile([P, PACK, N], BF16, name="planes", align_bytes=64)
+            for t in range(PACK):
+                c0 = b * PASS + t * P
+                x = psum.tile([P, N], F32, name="x", bufs=4)
+                nc.tensor.matmul_mx(
+                    out=x[:], lhsT=w4[:, 2 * c0 : 2 * (c0 + P)].bitcast(FP4X4), lhsT_scale=w4_sc[:, c0 : c0 + P],
+                    rhs=cat[0, j][:].bitcast(FP8X4), rhs_scale=cat_sc[j][:], start=True, stop=False,
+                )
+                nc.tensor.matmul_mx(
+                    out=x[:], lhsT=w1_q[b][:, t * P : (t + 1) * P].bitcast(FP8X4), lhsT_scale=w1_sc[b][:, t * P : (t + 1) * P],
+                    rhs=cat[1, j][:].bitcast(FP8X4), rhs_scale=cat_sc[j][4:P, :], start=False, stop=True,
+                )
+                th = work.tile([P, N], F32, name="th", bufs=8)
+                nc.scalar.activation(out=th[:], in_=x[:], func=ACT.Tanh)
+                nc.vector.scalar_tensor_tensor(
+                    out=planes[:, t, :], in0=th[:], scalar=gain_sb[:, b, t : t + 1], in1=hand_sb[j, b][:, t, :],
+                    op0=ALU.mult, op1=ALU.add,
+                )
+            woven = work.tile([P, N * PACK], BF16, name="woven", align_bytes=64)
+            for u in range(2):
+                nc.scalar.copy(
+                    out=woven[:, u * N * 2 : (u + 1) * N * 2].rearrange("p (c i t) -> p c t i", i=4, t=PACK),
+                    in_=planes[:, :, u * N // 2 : (u + 1) * N // 2].rearrange("p t (c i) -> p c t i", i=4),
+                )
+            return woven
+
+        def quantize_h(j, b, woven):
+            nc.vector.quantize_mx(out=h_q[j, b][:].bitcast(FP8X4), scales=h_sc[j, b][:], in_=woven[:])
+
+        def product(acc, m, rhs, rhs_scale):
+            cols = slice(m * P, (m + 1) * P)
+            for a in range(PASSES):
+                nc.tensor.matmul_mx(
+                    out=acc[:], lhsT=std[a][:, cols].bitcast(FP8X4), lhsT_scale=std_sc[4 * a : P, cols],
+                    rhs=rhs[a][:].bitcast(FP8X4), rhs_scale=rhs_scale[a], start=(a == 0), stop=(a == PASSES - 1),
+                )
+
+        def gate(j, m):
+            d = psum.tile([P, N], F32, name="d", bufs=2)
+            product(d, m, [cat[a, j] for a in range(PASSES)], [cat_sc[j][4 * a : P, :] for a in range(PASSES)])
+            g = work.tile([P, N], F32, name="g", bufs=3)
+            nc.scalar.activation(out=g[:], in_=d[:], func=ACT.Tanh, scale=0.5)
+            return g
+
+        def score(j, m, g):
+            e = psum.tile([P, N], F32, name="e", bufs=2)
+            product(e, m, [h_q[j, b] for b in range(PASSES)], [h_sc[j, b][:] for b in range(PASSES)])
+            gated = work.tile([P, N], F32, name="gated")
+            nc.vector.scalar_tensor_tensor(out=gated[:], in0=g[:], scalar=1.0, in1=e[:], op0=ALU.add, op1=ALU.mult)
+            y = work.tile([P, N], F32, name="y")
+            nc.scalar.activation(out=y[:], in_=gated[:], func=ACT.Identity, scale=0.5, bias=breed_sb[:, m : m + 1])
+            return y
+
+        def place(j, m, y):
+            nc.vector.tensor_tensor(
+                page[m][:].indirect(col_list[:, j * LIST_COLS : (j + 1) * LIST_COLS]), y[:], wgo_sb[j][:], ALU.mult
+            )
+            if j == HALVES - 1:
+                nc.sync.dma_start(out=out[m * P : (m + 1) * P, :], in_=page[m][:])
+
+        deal_w4_words()
+        for j in range(HALVES):
+            gather_cats(cat[0, j], cat_tab[0], j)
+        for j in range(HALVES):
+            gather_cats(cat_sc[j], cat_tab_sc, j)
+        deal_w4_scales()
+        for b in range(PASSES):
+            round_w1(b)
+            quantize_w1(b)
+        for j in range(HALVES):
+            gather_cats(cat[1, j], cat_tab[1], j)
+
+        woven_0 = features(0, 0)
+        gather_standards(std[0], std_tab[0])
+        gather_standards(std_sc, std_tab_sc)
+        woven_1 = features(0, 1)
+        gather_standards(std[1], std_tab[1])
+        quantize_h(0, 0, woven_0)
+        quantize_h(0, 1, woven_1)
+
+        ys = [score(0, m, gate(0, m)) for m in range(2)]
+        place(0, 0, ys[0])
+        place(0, 1, ys[1])
+        woven_a = features(1, 0)
+        y2 = score(0, 2, gate(0, 2))
+        place(0, 2, y2)
+        quantize_h(1, 0, woven_a)
+        woven_b = features(1, 1)
+        y3 = score(0, 3, gate(0, 3))
+        quantize_h(1, 1, woven_b)
+        y_next = score(1, 0, gate(1, 0))
+        place(0, 3, y3)
+        for m in range(M_TILES):
+            y_now = y_next
+            if m + 1 < M_TILES:
+                y_next = score(1, m + 1, gate(1, m + 1))
+            place(1, m, y_now)

@@ -37,8 +37,8 @@ def tile_list_steward_ring_scores_kernel(
         work = ctx.enter_context(tc.tile_pool(name="work", bufs=2))
         psum = ctx.enter_context(tc.psum_pool(name="psum", bufs=1))
 
-        def held(name, shape, dtype):
-            return keep.tile(shape, dtype, name=name, align_bytes=64)
+        def held(name, shape, dtype, tag=None):
+            return keep.tile(shape, dtype, name=name, tag=tag or name, align_bytes=64)
 
         cat_list = held("cat_list", [P, S // 16], U16)
         std_list = held("std_list", [P, S2 // 16], U16)
@@ -54,34 +54,32 @@ def tile_list_steward_ring_scores_kernel(
         w1_raw = [held("w1_raw%d" % b, [P, PACK, PASS], F32) for b in range(PASSES)]
         w1_bf = [held("w1_bf%d" % b, [P, PASS * PACK], BF16) for b in range(PASSES)]
         w1_q = [held("w1_q%d" % b, [P, PASS], U32) for b in range(PASSES)]
-        w1_sc = [held("w1_sc%d" % b, [P, PASS], U8) for b in range(PASSES)]
+        w1_sc = []
         gain_sb = held("gain_sb", [P, PASSES, PACK], F32)
         breed_sb = held("breed_sb", [P, M_TILES], F32)
         hand_sb = {(j, b): held("hand%d_%d" % (j, b), [P, PACK, N], F32) for j in range(HALVES) for b in range(PASSES)}
         wgo_sb = [held("wgo%d" % j, [P, N], F32) for j in range(HALVES)]
         page = [held("page%d" % m, [P, T2], F32) for m in range(M_TILES)]
-        cat = {(a, j): held("cat%d_%d" % (a, j), [P, N], U32) for a in range(PASSES) for j in range(HALVES)}
+        cat = [held("cat0", [P, S], U32)]
         cat_sc = [held("cat_sc%d" % j, [P, N], U8) for j in range(HALVES)]
-        std = [held("std%d" % a, [P, S2], U32) for a in range(PASSES)]
+        std = []
         std_sc = held("std_sc", [P, S2], U8)
         h_q = {(j, b): held("h_q%d_%d" % (j, b), [P, N], U32) for j in range(HALVES) for b in range(PASSES)}
         h_sc = {(j, b): held("h_sc%d_%d" % (j, b), [P, N], U8) for j in range(HALVES) for b in range(PASSES)}
 
+        def half(j):
+            return slice(j * N, (j + 1) * N)
+
         def load_words(tile, words):
             nc.sync.dma_start(out=tile[:].bitcast(I32), in_=words.rearrange("p t i -> p (t i)").bitcast(I32))
 
-        def load_scales(queue, tile, scales):
+        def load_scales(tile, scales):
             passes = scales.shape[0]
             for q in range(4):
-                queue.dma_start(
+                nc.gpsimd.dma_start(
                     out=tile[32 * q : 32 * q + 4 * passes, :].bitcast(I32),
                     in_=scales[:, 4 * q : 4 * q + 4, :].bitcast(I32),
                 )
-
-        def load_pass_scales(tile, scales, a):
-            for q in range(4):
-                row = 32 * q + 4 * a
-                nc.sync.dma_start(out=tile[row : row + 4, :].bitcast(I32), in_=scales[a, 4 * q : 4 * q + 4, :].bitcast(I32))
 
         def load_w1(b):
             nc.sync.dma_start(out=w1_raw[b][:], in_=w1[:, b * PASS : (b + 1) * PASS].rearrange("(p i) c -> p i c", i=PACK))
@@ -96,21 +94,18 @@ def tile_list_steward_ring_scores_kernel(
         def load_page(m):
             nc.sync.dma_start(out=page[m][:], in_=page1[m * P : (m + 1) * P, :])
 
-        nc.gpsimd.memset(cat_tab_sc[:, 0 : T // 2].bitcast(I32), 0)
-        nc.vector.memset(cat_tab_sc[:, T // 2 : T].bitcast(I32), 0)
-        for tile in (std_tab_sc, w4_raw_sc):
+        for tile in (cat_tab_sc, w4_raw_sc, std_tab_sc):
             nc.vector.memset(tile[:].bitcast(I32), 0)
+        load_scales(cat_tab_sc, tab_scales)
+        load_scales(w4_raw_sc, w4_scales)
+        load_scales(std_tab_sc, tab2_scales)
         nc.sync.dma_start(cat_list[:], offs)
         nc.sync.dma_start(out=w4_raw[:].bitcast(I32), in_=w4_words[0].bitcast(I32))
         load_words(cat_tab[0], tab_words[0])
-        load_pass_scales(cat_tab_sc, tab_scales, 0)
-        nc.sync.dma_start(out=gain_sb[:], in_=gain.rearrange("(b p t) -> p b t", b=PASSES, t=PACK))
-        load_scales(nc.gpsimd, std_tab_sc, tab2_scales)
         load_w1(0)
-        load_pass_scales(cat_tab_sc, tab_scales, 1)
         load_w1(1)
-        load_scales(nc.sync, w4_raw_sc, w4_scales)
         load_words(cat_tab[1], tab_words[1])
+        nc.sync.dma_start(out=gain_sb[:], in_=gain.rearrange("(b p t) -> p b t", b=PASSES, t=PACK))
         nc.sync.dma_start(std_list[:], offs2)
         load_words(std_tab[0], tab2_words[0])
         load_hand(0, 0)
@@ -130,8 +125,8 @@ def tile_list_steward_ring_scores_kernel(
 
         def deal_w4_words():
             nc.vector.tensor_copy(
-                out=w4[:].rearrange("p (b t q y) -> p b t q y", b=PASSES, t=PACK, y=2),
-                in_=w4_raw[:].rearrange("p (b q t y) -> p b t q y", b=PASSES, t=PACK, y=2),
+                out=w4[:].bitcast(U16).rearrange("p (b t q) -> p b t q", b=PASSES, t=PACK),
+                in_=w4_raw[:].bitcast(U16).rearrange("p (b q t) -> p b t q", b=PASSES, t=PACK),
             )
 
         def deal_w4_scales():
@@ -150,7 +145,7 @@ def tile_list_steward_ring_scores_kernel(
             nc.vector.quantize_mx(out=w1_q[b][:].bitcast(FP8X4), scales=w1_sc[b][:], in_=w1_bf[b][:])
 
         def gather_cats(dst, table, j):
-            nc.vector.tensor_copy(dst[:], table[:].indirect(cat_list[:, j * LIST_COLS : (j + 1) * LIST_COLS]))
+            nc.vector.tensor_copy(dst, table[:].indirect(cat_list[:, j * LIST_COLS : (j + 1) * LIST_COLS]))
 
         def gather_standards(dst, table):
             cols = STD_RUN // 16
@@ -159,18 +154,17 @@ def tile_list_steward_ring_scores_kernel(
                     dst[:, u * STD_RUN : (u + 1) * STD_RUN], table[:].indirect(std_list[:, u * cols : (u + 1) * cols])
                 )
 
-        def features(j, b):
-            planes = work.tile([P, PACK, N], BF16, name="planes", align_bytes=64)
+        def features(j, b, planes, woven=None):
             for t in range(PACK):
                 c0 = b * PASS + t * P
                 x = psum.tile([P, N], F32, name="x", bufs=4)
                 nc.tensor.matmul_mx(
                     out=x[:], lhsT=w4[:, 2 * c0 : 2 * (c0 + P)].bitcast(FP4X4), lhsT_scale=w4_sc[:, c0 : c0 + P],
-                    rhs=cat[0, j][:].bitcast(FP8X4), rhs_scale=cat_sc[j][:], start=True, stop=False,
+                    rhs=cat[0][:, half(j)].bitcast(FP8X4), rhs_scale=cat_sc[j][:], start=True, stop=False,
                 )
                 nc.tensor.matmul_mx(
                     out=x[:], lhsT=w1_q[b][:, t * P : (t + 1) * P].bitcast(FP8X4), lhsT_scale=w1_sc[b][:, t * P : (t + 1) * P],
-                    rhs=cat[1, j][:].bitcast(FP8X4), rhs_scale=cat_sc[j][4:P, :], start=False, stop=True,
+                    rhs=cat[1][:, half(j)].bitcast(FP8X4), rhs_scale=cat_sc[j][4:P, :], start=False, stop=True,
                 )
                 th = work.tile([P, N], F32, name="th", bufs=8)
                 nc.scalar.activation(out=th[:], in_=x[:], func=ACT.Tanh)
@@ -178,7 +172,8 @@ def tile_list_steward_ring_scores_kernel(
                     out=planes[:, t, :], in0=th[:], scalar=gain_sb[:, b, t : t + 1], in1=hand_sb[j, b][:, t, :],
                     op0=ALU.mult, op1=ALU.add,
                 )
-            woven = work.tile([P, N * PACK], BF16, name="woven", align_bytes=64)
+            if woven is None:
+                woven = work.tile([P, N * PACK], BF16, name="woven", align_bytes=64)
             for u in range(2):
                 nc.scalar.copy(
                     out=woven[:, u * N * 2 : (u + 1) * N * 2].rearrange("p (c i t) -> p c t i", i=4, t=PACK),
@@ -194,22 +189,24 @@ def tile_list_steward_ring_scores_kernel(
             for a in range(PASSES):
                 nc.tensor.matmul_mx(
                     out=acc[:], lhsT=std[a][:, cols].bitcast(FP8X4), lhsT_scale=std_sc[4 * a : P, cols],
-                    rhs=rhs[a][:].bitcast(FP8X4), rhs_scale=rhs_scale[a], start=(a == 0), stop=(a == PASSES - 1),
+                    rhs=rhs[a].bitcast(FP8X4), rhs_scale=rhs_scale[a], start=(a == 0), stop=(a == PASSES - 1),
                 )
 
         def gate(j, m):
             d = psum.tile([P, N], F32, name="d", bufs=2)
-            product(d, m, [cat[a, j] for a in range(PASSES)], [cat_sc[j][4 * a : P, :] for a in range(PASSES)])
+            product(d, m, [cat[a][:, half(j)] for a in range(PASSES)], [cat_sc[j][4 * a : P, :] for a in range(PASSES)])
             g = work.tile([P, N], F32, name="g", bufs=3)
             nc.scalar.activation(out=g[:], in_=d[:], func=ACT.Tanh, scale=0.5)
             return g
 
-        def score(j, m, g):
+        def score(j, m, g, y=None, gated=None):
             e = psum.tile([P, N], F32, name="e", bufs=2)
-            product(e, m, [h_q[j, b] for b in range(PASSES)], [h_sc[j, b][:] for b in range(PASSES)])
-            gated = work.tile([P, N], F32, name="gated")
+            product(e, m, [h_q[j, b][:] for b in range(PASSES)], [h_sc[j, b][:] for b in range(PASSES)])
+            if gated is None:
+                gated = work.tile([P, N], F32, name="gated")
             nc.vector.scalar_tensor_tensor(out=gated[:], in0=g[:], scalar=1.0, in1=e[:], op0=ALU.add, op1=ALU.mult)
-            y = work.tile([P, N], F32, name="y")
+            if y is None:
+                y = work.tile([P, N], F32, name="y", bufs=3)
             nc.scalar.activation(out=y[:], in_=gated[:], func=ACT.Identity, scale=0.5, bias=breed_sb[:, m : m + 1])
             return y
 
@@ -222,34 +219,37 @@ def tile_list_steward_ring_scores_kernel(
 
         deal_w4_words()
         for j in range(HALVES):
-            gather_cats(cat[0, j], cat_tab[0], j)
+            gather_cats(cat[0][:, half(j)], cat_tab[0], j)
         for j in range(HALVES):
-            gather_cats(cat_sc[j], cat_tab_sc, j)
+            gather_cats(cat_sc[j][:], cat_tab_sc, j)
         deal_w4_scales()
-        for b in range(PASSES):
+        for b, tag in enumerate(("w4_raw_sc", "w1_bf0")):
             round_w1(b)
+            w1_sc.append(held("w1_sc%d" % b, [P, PASS], U8, tag=tag))
             quantize_w1(b)
+        cat.append(held("cat1", [P, S], U32, tag="w1_bf1"))
         for j in range(HALVES):
-            gather_cats(cat[1, j], cat_tab[1], j)
+            gather_cats(cat[1][:, half(j)], cat_tab[1], j)
 
-        woven_0 = features(0, 0)
+        std.append(held("std0", [P, S2], U32, tag="cat_tab1"))
         gather_standards(std[0], std_tab[0])
         gather_standards(std_sc, std_tab_sc)
-        woven_1 = features(0, 1)
+        woven_0 = features(0, 0, held("planes00", [P, PACK, N], BF16, tag="std_tab_sc"))
+        std.append(held("std1", [P, S2], U32, tag="hand0_0"))
         gather_standards(std[1], std_tab[1])
+        woven_1 = features(0, 1, held("planes01", [P, PACK, N], BF16, tag="std_tab1"))
         quantize_h(0, 0, woven_0)
         quantize_h(0, 1, woven_1)
 
-        ys = [score(0, m, gate(0, m)) for m in range(2)]
+        ys = [score(0, 0, gate(0, 0), held("y00", [P, N], F32)), score(0, 1, gate(0, 1))]
         place(0, 0, ys[0])
         place(0, 1, ys[1])
-        woven_a = features(1, 0)
+        quantize_h(1, 0, features(1, 0, held("planes10", [P, PACK, N], BF16)))
         y2 = score(0, 2, gate(0, 2))
+        woven_b = features(1, 1, held("planes11", [P, PACK, N], BF16, tag="y00"), held("woven11", [P, N * PACK], BF16))
         place(0, 2, y2)
-        quantize_h(1, 0, woven_a)
-        woven_b = features(1, 1)
-        y3 = score(0, 3, gate(0, 3))
         quantize_h(1, 1, woven_b)
+        y3 = score(0, 3, gate(0, 3), gated=held("gated03", [P, N], F32, tag="woven11"))
         y_next = score(1, 0, gate(1, 0))
         place(0, 3, y3)
         for m in range(M_TILES):

@@ -24,7 +24,6 @@ N = 512
 HALVES = S // N
 M_TILES = S2 // P
 LIST_COLS = N // 16
-STD_RUN = 256
 
 
 def tile_list_steward_ring_scores_kernel(
@@ -61,7 +60,7 @@ def tile_list_steward_ring_scores_kernel(
         wgo_sb = [held("wgo%d" % j, [P, N], F32) for j in range(HALVES)]
         page = [held("page%d" % m, [P, T2], F32) for m in range(M_TILES)]
         cat = [held("cat0", [P, S], U32)]
-        cat_sc = [held("cat_sc%d" % j, [P, N], U8) for j in range(HALVES)]
+        cat_sc = held("cat_sc", [P, S], U8)
         std = []
         std_sc = held("std_sc", [P, S2], U8)
         h_q = {(j, b): held("h_q%d_%d" % (j, b), [P, N], U32) for j in range(HALVES) for b in range(PASSES)}
@@ -73,10 +72,10 @@ def tile_list_steward_ring_scores_kernel(
         def load_words(tile, words):
             nc.sync.dma_start(out=tile[:].bitcast(I32), in_=words.rearrange("p t i -> p (t i)").bitcast(I32))
 
-        def load_scales(tile, scales):
+        def load_scales(queue, tile, scales):
             passes = scales.shape[0]
             for q in range(4):
-                nc.gpsimd.dma_start(
+                queue.dma_start(
                     out=tile[32 * q : 32 * q + 4 * passes, :].bitcast(I32),
                     in_=scales[:, 4 * q : 4 * q + 4, :].bitcast(I32),
                 )
@@ -94,14 +93,16 @@ def tile_list_steward_ring_scores_kernel(
         def load_page(m):
             nc.sync.dma_start(out=page[m][:], in_=page1[m * P : (m + 1) * P, :])
 
-        for tile in (cat_tab_sc, w4_raw_sc, std_tab_sc):
+        nc.gpsimd.memset(w4_raw_sc[:].bitcast(I32), 0)
+        for tile in (cat_tab_sc, std_tab_sc):
             nc.vector.memset(tile[:].bitcast(I32), 0)
-        load_scales(cat_tab_sc, tab_scales)
-        load_scales(w4_raw_sc, w4_scales)
-        load_scales(std_tab_sc, tab2_scales)
+        load_scales(nc.gpsimd, cat_tab_sc, tab_scales)
+        load_scales(nc.gpsimd, std_tab_sc, tab2_scales)
         nc.sync.dma_start(cat_list[:], offs)
         nc.sync.dma_start(out=w4_raw[:].bitcast(I32), in_=w4_words[0].bitcast(I32))
         load_words(cat_tab[0], tab_words[0])
+        for r in range(4):
+            nc.sync.dma_start(out=w4_raw_sc[r:P:32, :].bitcast(I32), in_=w4_scales[0, r:16:4, :].bitcast(I32))
         load_w1(0)
         load_w1(1)
         load_words(cat_tab[1], tab_words[1])
@@ -148,38 +149,38 @@ def tile_list_steward_ring_scores_kernel(
             nc.vector.tensor_copy(dst, table[:].indirect(cat_list[:, j * LIST_COLS : (j + 1) * LIST_COLS]))
 
         def gather_standards(dst, table):
-            cols = STD_RUN // 16
-            for u in range(S2 // STD_RUN):
-                nc.vector.tensor_copy(
-                    dst[:, u * STD_RUN : (u + 1) * STD_RUN], table[:].indirect(std_list[:, u * cols : (u + 1) * cols])
-                )
+            nc.vector.tensor_copy(dst[:], table[:].indirect(std_list[:]))
 
-        def features(j, b, planes, woven=None):
+        def project(j, b, ths):
             for t in range(PACK):
                 c0 = b * PASS + t * P
                 x = psum.tile([P, N], F32, name="x", bufs=4)
                 nc.tensor.matmul_mx(
                     out=x[:], lhsT=w4[:, 2 * c0 : 2 * (c0 + P)].bitcast(FP4X4), lhsT_scale=w4_sc[:, c0 : c0 + P],
-                    rhs=cat[0][:, half(j)].bitcast(FP8X4), rhs_scale=cat_sc[j][:], start=True, stop=False,
+                    rhs=cat[0][:, half(j)].bitcast(FP8X4), rhs_scale=cat_sc[:, half(j)], start=True, stop=False,
                 )
                 nc.tensor.matmul_mx(
                     out=x[:], lhsT=w1_q[b][:, t * P : (t + 1) * P].bitcast(FP8X4), lhsT_scale=w1_sc[b][:, t * P : (t + 1) * P],
-                    rhs=cat[1][:, half(j)].bitcast(FP8X4), rhs_scale=cat_sc[j][4:P, :], start=False, stop=True,
+                    rhs=cat[1][:, half(j)].bitcast(FP8X4), rhs_scale=cat_sc[4:P, half(j)], start=False, stop=True,
                 )
-                th = work.tile([P, N], F32, name="th", bufs=8)
-                nc.scalar.activation(out=th[:], in_=x[:], func=ACT.Tanh)
+                nc.scalar.activation(out=ths[t], in_=x[:], func=ACT.Tanh)
+
+        def combine(j, b, ths, planes):
+            for t in range(PACK):
                 nc.vector.scalar_tensor_tensor(
-                    out=planes[:, t, :], in0=th[:], scalar=gain_sb[:, b, t : t + 1], in1=hand_sb[j, b][:, t, :],
+                    out=planes[:, t, :], in0=ths[t], scalar=gain_sb[:, b, t : t + 1], in1=hand_sb[j, b][:, t, :],
                     op0=ALU.mult, op1=ALU.add,
                 )
-            if woven is None:
-                woven = work.tile([P, N * PACK], BF16, name="woven", align_bytes=64)
+
+        def weave(planes, woven):
             for u in range(2):
                 nc.scalar.copy(
                     out=woven[:, u * N * 2 : (u + 1) * N * 2].rearrange("p (c i t) -> p c t i", i=4, t=PACK),
                     in_=planes[:, :, u * N // 2 : (u + 1) * N // 2].rearrange("p t (c i) -> p c t i", i=4),
                 )
-            return woven
+
+        def slots(tile):
+            return [tile[:, t, :] for t in range(tile.shape[1])]
 
         def quantize_h(j, b, woven):
             nc.vector.quantize_mx(out=h_q[j, b][:].bitcast(FP8X4), scales=h_sc[j, b][:], in_=woven[:])
@@ -192,11 +193,12 @@ def tile_list_steward_ring_scores_kernel(
                     rhs=rhs[a].bitcast(FP8X4), rhs_scale=rhs_scale[a], start=(a == 0), stop=(a == PASSES - 1),
                 )
 
-        def gate(j, m):
+        def gate(j, m, g=None):
             d = psum.tile([P, N], F32, name="d", bufs=2)
-            product(d, m, [cat[a][:, half(j)] for a in range(PASSES)], [cat_sc[j][4 * a : P, :] for a in range(PASSES)])
-            g = work.tile([P, N], F32, name="g", bufs=3)
-            nc.scalar.activation(out=g[:], in_=d[:], func=ACT.Tanh, scale=0.5)
+            product(d, m, [cat[a][:, half(j)] for a in range(PASSES)], [cat_sc[4 * a : P, half(j)] for a in range(PASSES)])
+            if g is None:
+                g = work.tile([P, N], F32, name="g", bufs=2)[:]
+            nc.scalar.activation(out=g, in_=d[:], func=ACT.Tanh, scale=0.5)
             return g
 
         def score(j, m, g, y=None, gated=None):
@@ -204,7 +206,7 @@ def tile_list_steward_ring_scores_kernel(
             product(e, m, [h_q[j, b][:] for b in range(PASSES)], [h_sc[j, b][:] for b in range(PASSES)])
             if gated is None:
                 gated = work.tile([P, N], F32, name="gated")
-            nc.vector.scalar_tensor_tensor(out=gated[:], in0=g[:], scalar=1.0, in1=e[:], op0=ALU.add, op1=ALU.mult)
+            nc.vector.scalar_tensor_tensor(out=gated[:], in0=g, scalar=1.0, in1=e[:], op0=ALU.add, op1=ALU.mult)
             if y is None:
                 y = work.tile([P, N], F32, name="y", bufs=3)
             nc.scalar.activation(out=y[:], in_=gated[:], func=ACT.Identity, scale=0.5, bias=breed_sb[:, m : m + 1])
@@ -218,12 +220,10 @@ def tile_list_steward_ring_scores_kernel(
                 nc.sync.dma_start(out=out[m * P : (m + 1) * P, :], in_=page[m][:])
 
         deal_w4_words()
-        for j in range(HALVES):
-            gather_cats(cat[0][:, half(j)], cat_tab[0], j)
-        for j in range(HALVES):
-            gather_cats(cat_sc[j][:], cat_tab_sc, j)
+        nc.vector.tensor_copy(cat[0][:], cat_tab[0][:].indirect(cat_list[:]))
+        nc.vector.tensor_copy(cat_sc[:], cat_tab_sc[:].indirect(cat_list[:]))
         deal_w4_scales()
-        for b, tag in enumerate(("w4_raw_sc", "w1_bf0")):
+        for b, tag in enumerate(("cat_tab_sc", "w1_bf0")):
             round_w1(b)
             w1_sc.append(held("w1_sc%d" % b, [P, PASS], U8, tag=tag))
             quantize_w1(b)
@@ -234,19 +234,45 @@ def tile_list_steward_ring_scores_kernel(
         std.append(held("std0", [P, S2], U32, tag="cat_tab1"))
         gather_standards(std[0], std_tab[0])
         gather_standards(std_sc, std_tab_sc)
-        woven_0 = features(0, 0, held("planes00", [P, PACK, N], BF16, tag="std_tab_sc"))
+        th00 = slots(held("th00", [P, PACK, N], F32))
+        th01 = slots(held("th01", [P, PACK, N], F32))
+        project(0, 0, th00)
+        project(0, 1, th01)
+        planes00 = held("planes00", [P, PACK, N], BF16, tag="std_tab_sc")
+        combine(0, 0, th00, planes00)
         std.append(held("std1", [P, S2], U32, tag="hand0_0"))
         gather_standards(std[1], std_tab[1])
-        woven_1 = features(0, 1, held("planes01", [P, PACK, N], BF16, tag="std_tab1"))
-        quantize_h(0, 0, woven_0)
-        quantize_h(0, 1, woven_1)
+        woven00 = held("woven00", [P, N * PACK], BF16)
+        weave(planes00, woven00)
+        planes01 = held("planes01", [P, PACK, N], BF16, tag="std_tab1")
+        combine(0, 1, th01, planes01)
+        th10 = slots(held("th10", [P, PACK, N], F32, tag="std_tab_sc"))
+        project(1, 0, th10)
+        woven01 = held("woven01", [P, N * PACK], BF16)
+        weave(planes01, woven01)
+        quantize_h(0, 0, woven00)
+        quantize_h(0, 1, woven01)
 
-        ys = [score(0, 0, gate(0, 0), held("y00", [P, N], F32)), score(0, 1, gate(0, 1))]
+        g01 = held("g01", [P, 2, N], F32, tag="std_tab1")
+        gates = [gate(0, m, g01[:, m, :]) for m in range(2)]
+        ys = [
+            score(0, 0, gates[0], held("y00", [P, N], F32), held("gated00", [P, N], F32)),
+            score(0, 1, gates[1], None, held("gated01", [P, N], F32)),
+        ]
         place(0, 0, ys[0])
         place(0, 1, ys[1])
-        quantize_h(1, 0, features(1, 0, held("planes10", [P, PACK, N], BF16)))
-        y2 = score(0, 2, gate(0, 2))
-        woven_b = features(1, 1, held("planes11", [P, PACK, N], BF16, tag="y00"), held("woven11", [P, N * PACK], BF16))
+        planes10 = held("planes10", [P, PACK, N], BF16)
+        combine(1, 0, th10, planes10)
+        woven10 = held("woven10", [P, N * PACK], BF16, tag="gated00")
+        weave(planes10, woven10)
+        quantize_h(1, 0, woven10)
+        th11 = slots(held("th11a", [P, 2, N], F32, tag="gated01")) + slots(held("th11b", [P, 2, N], F32, tag="std_tab1"))
+        project(1, 1, th11)
+        planes11 = held("planes11", [P, PACK, N], BF16, tag="y00")
+        combine(1, 1, th11, planes11)
+        woven_b = held("woven11", [P, N * PACK], BF16)
+        weave(planes11, woven_b)
+        y2 = score(0, 2, gate(0, 2), held("y02", [P, N], F32, tag="gated01"))
         place(0, 2, y2)
         quantize_h(1, 1, woven_b)
         y3 = score(0, 3, gate(0, 3), gated=held("gated03", [P, N], F32, tag="woven11"))

@@ -110,8 +110,8 @@ def tile_list_steward_ring_scores_kernel(
         nc.sync.dma_start(std_list[:], offs2)
         load_words(std_tab[0], tab2_words[0])
         load_hand(0, 0)
-        load_words(std_tab[1], tab2_words[1])
         load_hand(0, 1)
+        load_words(std_tab[1], tab2_words[1])
         load_hand(1, 0)
         nc.sync.dma_start(col_list[:], offs3)
         load_wgo(0)
@@ -240,17 +240,20 @@ def tile_list_steward_ring_scores_kernel(
         project(0, 1, th01)
         planes00 = held("planes00", [P, PACK, N], BF16, tag="std_tab_sc")
         combine(0, 0, th00, planes00)
-        std.append(held("std1", [P, S2], U32, tag="hand0_0"))
-        gather_standards(std[1], std_tab[1])
         woven00 = held("woven00", [P, N * PACK], BF16)
         weave(planes00, woven00)
-        planes01 = held("planes01", [P, PACK, N], BF16, tag="std_tab1")
+        planes01 = held("planes01", [P, PACK, N], BF16, tag="w1_raw0")
         combine(0, 1, th01, planes01)
         th10 = slots(held("th10", [P, PACK, N], F32, tag="std_tab_sc"))
         project(1, 0, th10)
-        woven01 = held("woven01", [P, N * PACK], BF16)
-        weave(planes01, woven01)
         quantize_h(0, 0, woven00)
+        woven01 = held("woven01", [P, N * PACK], BF16)
+        nc.vector.tensor_copy(
+            out=woven01[:].rearrange("p (c i t) -> p c t i", i=4, t=PACK),
+            in_=planes01[:].rearrange("p t (c i) -> p c t i", i=4),
+        )
+        std.append(held("std1", [P, S2], U32, tag="w1_raw0"))
+        gather_standards(std[1], std_tab[1])
         quantize_h(0, 1, woven01)
 
         g01 = held("g01", [P, 2, N], F32, tag="std_tab1")

from contextlib import ExitStack

import concourse.mybir as mybir

K, KB, T, S, H, T3, S2, T2 = 1024, 512, 4096, 1024, 1024, 2048, 512, 2048
FLOPS = 2 * K * H * S + 2 * 2 * H * S2 * S

F32 = mybir.dt.float32
BF16 = mybir.dt.bfloat16
I32 = mybir.dt.int32
U32 = mybir.dt.uint32
U16 = mybir.dt.uint16
U8 = mybir.dt.uint8
FP8X4 = mybir.dt.float8_e4m3fn_x4
FP4X4 = mybir.dt.float4_e2m1fn_x4
ACT = mybir.ActivationFunctionType
ALU = mybir.AluOpType

P = 128
PACK = 4
PASS = P * PACK
PASSES = 2
N = 512
HALVES = S // N
M_TILES = S2 // P
LIST_COLS = N // 16


def tile_list_steward_ring_scores_kernel(
    tc, tab_words, tab_scales, offs, tab2_words, tab2_scales, offs2, offs3,
    w4_words, w4_scales, w1, gain, hand, breed, wgo, page1, out,
):
    nc = tc.nc
    with ExitStack() as ctx:
        keep = ctx.enter_context(tc.tile_pool(name="keep", bufs=1))
        work = ctx.enter_context(tc.tile_pool(name="work", bufs=2))
        psum = ctx.enter_context(tc.psum_pool(name="psum", bufs=1))

        def held(name, shape, dtype, tag=None):
            return keep.tile(shape, dtype, name=name, tag=tag or name, align_bytes=64)

        cat_list = held("cat_list", [P, S // 16], U16)
        std_list = held("std_list", [P, S2 // 16], U16)
        col_list = held("col_list", [P, S // 16], U16)
        cat_tab = [held("cat_tab%d" % a, [P, T], U32) for a in range(PASSES)]
        cat_tab_sc = held("cat_tab_sc", [P, T], U8)
        std_tab = [held("std_tab%d" % a, [P, T3], U32) for a in range(PASSES)]
        std_tab_sc = held("std_tab_sc", [P, T3], U8)
        w4_raw = held("w4_raw", [P, 2 * H], U8)
        w4_raw_sc = held("w4_raw_sc", [P, H], U8)
        w4 = held("w4", [P, 2 * H], U8)
        w4_sc = held("w4_sc", [P, H], U8)
        w1_raw = [held("w1_raw%d" % b, [P, PACK, PASS], F32) for b in range(PASSES)]
        w1_bf = [held("w1_bf%d" % b, [P, PASS * PACK], BF16) for b in range(PASSES)]
        w1_q = [held("w1_q%d" % b, [P, PASS], U32) for b in range(PASSES)]
        w1_sc = []
        gain_sb = held("gain_sb", [P, PASSES, PACK], F32)
        breed_sb = held("breed_sb", [P, M_TILES], F32)
        hand_sb = {(j, b): held("hand%d_%d" % (j, b), [P, PACK, N], F32) for j in range(HALVES) for b in range(PASSES)}
        wgo_sb = [held("wgo%d" % j, [P, N], F32) for j in range(HALVES)]
        page = [held("page%d" % m, [P, T2], F32) for m in range(M_TILES)]
        cat = [held("cat0", [P, S], U32)]
        cat_sc = held("cat_sc", [P, S], U8)
        std = []
        std_sc = held("std_sc", [P, S2], U8)
        h_q = {(j, b): held("h_q%d_%d" % (j, b), [P, N], U32) for j in range(HALVES) for b in range(PASSES)}
        h_sc = {(j, b): held("h_sc%d_%d" % (j, b), [P, N], U8) for j in range(HALVES) for b in range(PASSES)}

        def half(j):
            return slice(j * N, (j + 1) * N)

        def load_words(tile, words):
            nc.sync.dma_start(out=tile[:].bitcast(I32), in_=words.rearrange("p t i -> p (t i)").bitcast(I32))

        def load_scales(queue, tile, scales):
            passes = scales.shape[0]
            for q in range(4):
                queue.dma_start(
                    out=tile[32 * q : 32 * q + 4 * passes, :].bitcast(I32),
                    in_=scales[:, 4 * q : 4 * q + 4, :].bitcast(I32),
                )

        def load_w1(b):
            nc.sync.dma_start(out=w1_raw[b][:], in_=w1[:, b * PASS : (b + 1) * PASS].rearrange("(p i) c -> p i c", i=PACK))

        def load_hand(j, b):
            rows = hand[b * PASS : (b + 1) * PASS, j * N : (j + 1) * N]
            nc.sync.dma_start(out=hand_sb[j, b][:], in_=rows.rearrange("(p t) n -> p t n", t=PACK))

        def load_wgo(j):
            nc.sync.dma_start(out=wgo_sb[j][:], in_=wgo[:, j * N : (j + 1) * N])

        def load_page(m):
            nc.sync.dma_start(out=page[m][:], in_=page1[m * P : (m + 1) * P, :])

        nc.gpsimd.memset(w4_raw_sc[:].bitcast(I32), 0)
        for tile in (cat_tab_sc, std_tab_sc):
            nc.vector.memset(tile[:].bitcast(I32), 0)
        load_scales(nc.gpsimd, cat_tab_sc, tab_scales)
        load_scales(nc.gpsimd, std_tab_sc, tab2_scales)
        nc.sync.dma_start(cat_list[:], offs)
        nc.sync.dma_start(out=w4_raw[:].bitcast(I32), in_=w4_words[0].bitcast(I32))
        load_words(cat_tab[0], tab_words[0])
        for r in range(4):
            nc.sync.dma_start(out=w4_raw_sc[r:P:32, :].bitcast(I32), in_=w4_scales[0, r:16:4, :].bitcast(I32))
        load_w1(0)
        load_w1(1)
        load_words(cat_tab[1], tab_words[1])
        nc.sync.dma_start(out=gain_sb[:], in_=gain.rearrange("(b p t) -> p b t", b=PASSES, t=PACK))
        nc.sync.dma_start(std_list[:], offs2)
        load_words(std_tab[0], tab2_words[0])
        load_hand(0, 0)
        load_hand(0, 1)
        load_words(std_tab[1], tab2_words[1])
        load_hand(1, 0)
        nc.sync.dma_start(col_list[:], offs3)
        load_wgo(0)
        with nc.allow_non_contiguous_dma(reason="one bias value a partition"):
            nc.sync.dma_start(out=breed_sb[:], in_=breed.rearrange("(m p) -> p m", p=P))
        load_page(0)
        load_page(1)
        load_hand(1, 1)
        load_page(2)
        load_page(3)
        load_wgo(1)

        def deal_w4_words():
            nc.vector.tensor_copy(
                out=w4[:].bitcast(U16).rearrange("p (b t q) -> p b t q", b=PASSES, t=PACK),
                in_=w4_raw[:].bitcast(U16).rearrange("p (b q t) -> p b t q", b=PASSES, t=PACK),
            )

        def deal_w4_scales():
            nc.vector.tensor_copy(
                out=w4_sc[:].rearrange("p (b t q) -> p b t q", b=PASSES, t=PACK),
                in_=w4_raw_sc[:].rearrange("p (b q t) -> p b t q", b=PASSES, t=PACK),
            )

        def round_w1(b):
            nc.scalar.copy(
                out=w1_bf[b][:].rearrange("p (t q i) -> p q t i", t=PACK, i=PACK),
                in_=w1_raw[b][:].rearrange("p i (q t) -> p q t i", t=PACK),
            )

        def quantize_w1(b):
            nc.vector.quantize_mx(out=w1_q[b][:].bitcast(FP8X4), scales=w1_sc[b][:], in_=w1_bf[b][:])

        def gather_cats(dst, table, j):
            nc.vector.tensor_copy(dst, table[:].indirect(cat_list[:, j * LIST_COLS : (j + 1) * LIST_COLS]))

        def gather_standards(dst, table):
            nc.vector.tensor_copy(dst[:], table[:].indirect(std_list[:]))

        def project(j, b, ths):
            for t in range(PACK):
                c0 = b * PASS + t * P
                x = psum.tile([P, N], F32, name="x", bufs=4)
                nc.tensor.matmul_mx(
                    out=x[:], lhsT=w4[:, 2 * c0 : 2 * (c0 + P)].bitcast(FP4X4), lhsT_scale=w4_sc[:, c0 : c0 + P],
                    rhs=cat[0][:, half(j)].bitcast(FP8X4), rhs_scale=cat_sc[:, half(j)], start=True, stop=False,
                )
                nc.tensor.matmul_mx(
                    out=x[:], lhsT=w1_q[b][:, t * P : (t + 1) * P].bitcast(FP8X4), lhsT_scale=w1_sc[b][:, t * P : (t + 1) * P],
                    rhs=cat[1][:, half(j)].bitcast(FP8X4), rhs_scale=cat_sc[4:P, half(j)], start=False, stop=True,
                )
                nc.scalar.activation(out=ths[t], in_=x[:], func=ACT.Tanh)

        def combine(j, b, ths, planes):
            for t in range(PACK):
                nc.vector.scalar_tensor_tensor(
                    out=planes[:, t, :], in0=ths[t], scalar=gain_sb[:, b, t : t + 1], in1=hand_sb[j, b][:, t, :],
                    op0=ALU.mult, op1=ALU.add,
                )

        def weave(planes, woven):
            for u in range(2):
                nc.scalar.copy(
                    out=woven[:, u * N * 2 : (u + 1) * N * 2].rearrange("p (c i t) -> p c t i", i=4, t=PACK),
                    in_=planes[:, :, u * N // 2 : (u + 1) * N // 2].rearrange("p t (c i) -> p c t i", i=4),
                )

        def slots(tile):
            return [tile[:, t, :] for t in range(tile.shape[1])]

        def quantize_h(j, b, woven):
            nc.vector.quantize_mx(out=h_q[j, b][:].bitcast(FP8X4), scales=h_sc[j, b][:], in_=woven[:])

        def product(acc, m, rhs, rhs_scale):
            cols = slice(m * P, (m + 1) * P)
            for a in range(PASSES):
                nc.tensor.matmul_mx(
                    out=acc[:], lhsT=std[a][:, cols].bitcast(FP8X4), lhsT_scale=std_sc[4 * a : P, cols],
                    rhs=rhs[a].bitcast(FP8X4), rhs_scale=rhs_scale[a], start=(a == 0), stop=(a == PASSES - 1),
                )

        def gate(j, m, g=None):
            d = psum.tile([P, N], F32, name="d", bufs=2)
            product(d, m, [cat[a][:, half(j)] for a in range(PASSES)], [cat_sc[4 * a : P, half(j)] for a in range(PASSES)])
            if g is None:
                g = work.tile([P, N], F32, name="g", bufs=2)[:]
            nc.scalar.activation(out=g, in_=d[:], func=ACT.Tanh, scale=0.5)
            return g

        def score(j, m, g, y=None, gated=None):
            e = psum.tile([P, N], F32, name="e", bufs=2)
            product(e, m, [h_q[j, b][:] for b in range(PASSES)], [h_sc[j, b][:] for b in range(PASSES)])
            if gated is None:
                gated = work.tile([P, N], F32, name="gated")
            nc.vector.scalar_tensor_tensor(out=gated[:], in0=g, scalar=1.0, in1=e[:], op0=ALU.add, op1=ALU.mult)
            if y is None:
                y = work.tile([P, N], F32, name="y", bufs=3)
            nc.scalar.activation(out=y[:], in_=gated[:], func=ACT.Identity, scale=0.5, bias=breed_sb[:, m : m + 1])
            return y

        def place(j, m, y):
            nc.vector.tensor_tensor(
                page[m][:].indirect(col_list[:, j * LIST_COLS : (j + 1) * LIST_COLS]), y[:], wgo_sb[j][:], ALU.mult
            )
            if j == HALVES - 1:
                nc.sync.dma_start(out=out[m * P : (m + 1) * P, :], in_=page[m][:])

        deal_w4_words()
        nc.vector.tensor_copy(cat[0][:], cat_tab[0][:].indirect(cat_list[:]))
        nc.vector.tensor_copy(cat_sc[:], cat_tab_sc[:].indirect(cat_list[:]))
        deal_w4_scales()
        for b, tag in enumerate(("cat_tab_sc", "w1_bf0")):
            round_w1(b)
            w1_sc.append(held("w1_sc%d" % b, [P, PASS], U8, tag=tag))
            quantize_w1(b)
        cat.append(held("cat1", [P, S], U32, tag="w1_bf1"))
        for j in range(HALVES):
            gather_cats(cat[1][:, half(j)], cat_tab[1], j)

        std.append(held("std0", [P, S2], U32, tag="cat_tab1"))
        gather_standards(std[0], std_tab[0])
        gather_standards(std_sc, std_tab_sc)
        th00 = slots(held("th00", [P, PACK, N], F32))
        th01 = slots(held("th01", [P, PACK, N], F32))
        project(0, 0, th00)
        project(0, 1, th01)
        planes00 = held("planes00", [P, PACK, N], BF16, tag="std_tab_sc")
        combine(0, 0, th00, planes00)
        woven00 = held("woven00", [P, N * PACK], BF16)
        weave(planes00, woven00)
        planes01 = held("planes01", [P, PACK, N], BF16, tag="w1_raw0")
        combine(0, 1, th01, planes01)
        th10 = slots(held("th10", [P, PACK, N], F32, tag="std_tab_sc"))
        project(1, 0, th10)
        quantize_h(0, 0, woven00)
        woven01 = held("woven01", [P, N * PACK], BF16)
        nc.vector.tensor_copy(
            out=woven01[:].rearrange("p (c i t) -> p c t i", i=4, t=PACK),
            in_=planes01[:].rearrange("p t (c i) -> p c t i", i=4),
        )
        std.append(held("std1", [P, S2], U32, tag="w1_raw0"))
        gather_standards(std[1], std_tab[1])
        quantize_h(0, 1, woven01)

        g01 = held("g01", [P, 2, N], F32, tag="std_tab1")
        gates = [gate(0, m, g01[:, m, :]) for m in range(2)]
        ys = [
            score(0, 0, gates[0], held("y00", [P, N], F32), held("gated00", [P, N], F32)),
            score(0, 1, gates[1], None, held("gated01", [P, N], F32)),
        ]
        place(0, 0, ys[0])
        place(0, 1, ys[1])
        planes10 = held("planes10", [P, PACK, N], BF16)
        combine(1, 0, th10, planes10)
        woven10 = held("woven10", [P, N * PACK], BF16, tag="gated00")
        weave(planes10, woven10)
        quantize_h(1, 0, woven10)
        th11 = slots(held("th11a", [P, 2, N], F32, tag="gated01")) + slots(held("th11b", [P, 2, N], F32, tag="std_tab1"))
        project(1, 1, th11)
        planes11 = held("planes11", [P, PACK, N], BF16, tag="y00")
        combine(1, 1, th11, planes11)
        woven_b = held("woven11", [P, N * PACK], BF16)
        weave(planes11, woven_b)
        y2 = score(0, 2, gate(0, 2), held("y02", [P, N], F32, tag="gated01"))
        place(0, 2, y2)
        quantize_h(1, 1, woven_b)
        y3 = score(0, 3, gate(0, 3), gated=held("gated03", [P, N], F32, tag="woven11"))
        y_next = score(1, 0, gate(1, 0))
        place(0, 3, y3)
        for m in range(M_TILES):
            y_now = y_next
            if m + 1 < M_TILES:
                y_next = score(1, m + 1, gate(1, m + 1))
            place(1, m, y_now)
